import numpy as np
import ml_dtypes


def mxq(x, axis, fmt="e4m3"):
    dtype, down = {"e4m3": (ml_dtypes.float8_e4m3fn, 7), "e5m2": (ml_dtypes.float8_e5m2, 14)}[fmt]
    v = np.moveaxis(np.asarray(x, np.float32).astype(ml_dtypes.bfloat16).astype(np.float64), axis, -1)
    blocks = v.reshape(v.shape[:-1] + (-1, 32))
    amax = np.abs(blocks).max(-1, keepdims=True)
    byte = np.maximum(np.where(amax > 0, np.frexp(amax)[1] - 1 + 127, 0) - down, 1)
    scale = np.exp2(byte - 127.0)
    codes = (blocks / scale).astype(np.float32).astype(dtype).astype(np.float64)
    return np.moveaxis((codes * scale).reshape(v.shape), -1, axis)


WIDE = False


def mx_kscale(k):
    if not WIDE:
        return np.ones(k)
    levels = np.array([10, -10, 5, -5, 0])
    if k % 512:
        return np.exp2(np.random.permutation(np.resize(levels, k // 32))).repeat(32)
    a = np.empty((k // 512, 16))
    for p in range(k // 512):
        a[p, :8] = np.random.permutation(np.resize(levels, 8))
        for g in range(8):
            far = levels[np.abs(levels - a[p, g]) >= 10]
            a[p, g + 8] = far[np.random.randint(len(far))]
    return np.exp2(a.ravel()).repeat(32)


BF16 = ml_dtypes.bfloat16


def bf(x):
    return np.asarray(x, np.float32).astype(BF16)


def f64(x):
    return np.asarray(x).astype(np.float64)


M, K, N, R = 2048, 1024, 1024, 1024
OMEGA1, OMEGA2 = 1.5, 2.0


def draw0():
    s, u = mx_kscale(K), mx_kscale(M)
    return {"x": bf(np.random.standard_normal((M, K)) * s),
            "w": bf(np.random.standard_normal((K, N)) / np.sqrt(K) / s[:, None]),
            "b": bf(0.3 * np.random.standard_normal(N)),
            "freq1": bf(OMEGA1 * (1 + 0.1 * np.random.standard_normal(N))),
            "amp": bf(np.exp(0.3 * np.random.standard_normal(M)) * u),
            "p": bf(np.random.standard_normal((R, M)) / np.sqrt(M) / u),
            "c": bf(0.3 * np.random.standard_normal(N)),
            "freq2": bf(OMEGA2 * (1 + 0.1 * np.random.standard_normal(N)))}


def core(x, w, b, freq1, amp, p, c, freq2):
    y = mxq(f64(x), 1, "e4m3") @ mxq(f64(w), 0, "e4m3")
    h = f64(amp)[:, None] * np.sin(f64(freq1) * (y + f64(b)))
    z = mxq(f64(p), 1, "e4m3") @ mxq(h, 0, "e4m3")
    return np.sin(f64(freq2) * (z + f64(c)))


def e4m3fn_bytes(y):
    return np.clip(np.asarray(y, np.float64), -448.0, 448.0).astype(np.float32).astype(ml_dtypes.float8_e4m3fn).view(np.uint8)


def e4m3fn_values(b):
    return np.asarray(b, np.uint8).view(ml_dtypes.float8_e4m3fn).astype(np.float64)


def setup_inputs():
    d = draw0()
    x0 = np.asarray(d['x']).astype(np.float64)
    s = (np.max(np.abs(x0), axis=(0,), keepdims=True) / 448.0).astype(np.float32)
    out = {}
    for k, v in d.items():
        if k == 'x':
            out['x_bytes'] = e4m3fn_bytes(x0 / s.astype(np.float64))
            out['x_scale'] = s
        else:
            out[k] = v
    return out


def reference(x_bytes, x_scale, w, b, freq1, amp, p, c, freq2):
    return core(e4m3fn_values(x_bytes) * x_scale.astype(np.float64), w, b, freq1, amp, p, c, freq2)

from contextlib import ExitStack
import math

import concourse.mybir as mybir
from concourse.masks import make_identity

M, K, N, R = 2048, 1024, 1024, 1024
FLOPS = 2 * M * K * N + 2 * R * M * N

F32 = mybir.dt.float32
BF16 = mybir.dt.bfloat16
I32 = mybir.dt.int32
U32 = mybir.dt.uint32
U8 = mybir.dt.uint8
FP8 = mybir.dt.float8_e4m3fn
FP8X4 = mybir.dt.float8_e4m3fn_x4
ACT = mybir.ActivationFunctionType
OP = mybir.AluOpType

P = 128
PACK = 4
TWO_PI = 2.0 * math.pi
GROUP0 = 4


def tile_siren_anchor_field_f4_kernel(tc, x_bytes, x_scale, w, b, freq1, amp, p, c, freq2, out):
    nc = tc.nc
    with ExitStack() as ctx:
        keep = ctx.enter_context(tc.tile_pool(name="keep", bufs=1))
        stage = ctx.enter_context(tc.tile_pool(name="stage", bufs=2))
        psum = ctx.enter_context(tc.psum_pool(name="psum", bufs=2))

        x_view = x_bytes.rearrange("(j q t) k -> j q t k", q=P, t=PACK)
        xb = []
        for j in range(4):
            xb.append(keep.tile([P, PACK, K], U8, name=f"xb{j}", align_bytes=64))
        nc.sync.dma_start(out=xb[0][:], in_=x_view[0])
        xs_sc = keep.tile([P, K], F32, name="xs_sc")
        nc.scalar.dma_start(out=xs_sc[:], in_=x_scale.rearrange("o k -> (o k)").partition_broadcast(P))
        vrows = keep.tile([P, P], BF16, name="vrows")
        nc.vector.memset(vrows[:], 0.0)
        w_view = w.rearrange("(g q t) n -> g q t n", q=P, t=PACK)
        wraw = []
        for g in range(2):
            wraw.append(keep.tile([P, PACK, N], BF16, name=f"wraw{g}", align_bytes=64))
        nc.sync.dma_start(out=wraw[0][:], in_=w_view[0])
        nc.sync.dma_start(out=wraw[1][:], in_=w_view[1])
        for q, vec in enumerate((freq1, b, freq2, c)):
            nc.sync.dma_start(out=vrows[8 * q : 8 * q + 8, :], in_=vec.rearrange("(i q) -> i q", q=P))
        amp_sb = keep.tile([P, 4, PACK], BF16, name="amp_sb")
        nc.sync.dma_start(out=amp_sb[:], in_=amp.rearrange("(j q t) -> q j t", q=P, t=PACK))
        for j in range(1, 4):
            nc.sync.dma_start(out=xb[j][:], in_=x_view[j])
        praw = []
        for rt in range(8):
            praw.append(keep.tile([P, M], BF16, name=f"praw{rt}", align_bytes=64))
            nc.sync.dma_start(out=praw[rt][:], in_=p[rt * P : (rt + 1) * P, :])

        warm = keep.tile([P, 1], F32, name="warm")
        nc.vector.memset(warm[:], 0.0)
        nc.scalar.activation(out=warm[:], in_=warm[:], func=ACT.Sin)
        ident_b = keep.tile([P, P], BF16, name="ident_b")
        make_identity(nc, ident_b[:])
        ident_f = keep.tile([P, P], F32, name="ident_f")
        make_identity(nc, ident_f[:])

        vt = psum.tile([P, P], BF16, name="vt", tag="tx", bufs=3)
        nc.tensor.transpose(vt[:], vrows[:], ident_b[:])
        f1 = keep.tile([P, 8], F32, name="f1")
        fb1 = keep.tile([P, 8], F32, name="fb1")
        b1 = keep.tile([P, 8], F32, name="b1")
        f2 = keep.tile([P, 8], F32, name="f2")
        b2 = keep.tile([P, 8], F32, name="b2")
        vs = keep.tile([P, 32], F32, name="vs")
        nc.vector.tensor_copy(out=vs[:], in_=vt[:, 0:32])
        nc.vector.tensor_scalar(f1[:], vs[:, 0:8], 1.0 / TWO_PI, None, OP.mult)
        nc.vector.tensor_tensor(fb1[:], vs[:, 0:8], vs[:, 8:16], OP.mult)
        nc.vector.tensor_scalar(b1[:], fb1[:], 1.0 / TWO_PI, None, OP.mult)
        nc.vector.tensor_scalar(f2[:], vs[:, 16:24], 1.0 / TWO_PI, None, OP.mult)
        nc.vector.tensor_tensor(b2[:], f2[:], vs[:, 24:32], OP.mult)

        xq = keep.tile([P, 4, 2, 512], U32, name="xq", align_bytes=64)
        xqs = keep.tile([P, 4, 2, 512], U8, name="xqs", align_bytes=64)
        wq = keep.tile([P, 2, N], U32, name="wq", align_bytes=64)
        wqs = keep.tile([P, 2, N], U8, name="wqs", align_bytes=64)
        pq = keep.tile([P, 4, R], U32, name="pq", align_bytes=64)
        pqs = keep.tile([P, 4, R], U8, name="pqs", align_bytes=64)
        hq = keep.tile([P, 4, N], U32, name="hq", align_bytes=64)
        hqs = keep.tile([P, 4, N], U8, name="hqs", align_bytes=64)

        def w_prep(q):
            cols = slice(256 * q, 256 * q + 256)
            for g in range(2):
                wi = stage.tile([P, 256, PACK], BF16, name="wi", align_bytes=64, bufs=2)
                nc.scalar.copy(out=wi[:], in_=wraw[g][:, :, cols].rearrange("q t n -> q n t"))
                nc.vector.quantize_mx(
                    out=wq[:, g, cols].bitcast(FP8X4),
                    scales=wqs[:, g, cols],
                    in_=wi[:].rearrange("q n t -> q (n t)"),
                )

        xs = {}
        xi = {}

        def x_mult(j, t):
            if t == 0:
                xs[j] = stage.tile([P, PACK, K], BF16, name="xs", align_bytes=64, bufs=2)
            nc.vector.tensor_tensor(xs[j][:, t, :], xb[j][:, t, :].bitcast(FP8), xs_sc[:], OP.mult)

        def x_turn(j, t):
            if t == 0:
                xi[j] = stage.tile([P, 2, 512, PACK], BF16, name="xi", align_bytes=64, bufs=2)
            bank = psum.tile([P, 2, 2, P], F32, name="bank", tag="tx", bufs=3)
            words = xs[j][:, t, :].bitcast(F32)
            for g in range(2):
                for u in range(2):
                    nc.tensor.transpose(bank[:, g, u, :], words[:, 256 * g + u : 256 * (g + 1) : 2], ident_f[:])
            dst = xi[j][:].bitcast(F32)[:, :, t * P : (t + 1) * P, :]
            nc.scalar.copy(out=dst, in_=bank[:].rearrange("q g u r -> q g r u"))

        def x_quant(j, g):
            nc.vector.quantize_mx(
                out=xq[:, j, g, :].bitcast(FP8X4),
                scales=xqs[:, j, g, :],
                in_=xi[j][:, g].rearrange("q m t -> q (m t)"),
            )

        pi = {}

        def p_turn(half, jp, rr):
            if rr == 0:
                pi[half, jp] = stage.tile([P, 2, 512, PACK], BF16, name="pi", align_bytes=64, bufs=2)
            bank = psum.tile([P, 2, 2, P], F32, name="bank", tag="tx", bufs=3)
            words = praw[4 * half + rr][:].bitcast(F32)
            for jj in range(2):
                j = 2 * jp + jj
                for u in range(2):
                    nc.tensor.transpose(bank[:, jj, u, :], words[:, 256 * j + u : 256 * (j + 1) : 2], ident_f[:])
            dst = pi[half, jp][:].bitcast(F32)[:, :, rr * P : (rr + 1) * P, :]
            nc.scalar.copy(out=dst, in_=bank[:].rearrange("q g u r -> q g r u"))
            if rr == 3:
                for jj in range(2):
                    j = 2 * jp + jj
                    nc.vector.quantize_mx(
                        out=pq[:, j, half * 512 : half * 512 + 512].bitcast(FP8X4),
                        scales=pqs[:, j, half * 512 : half * 512 + 512],
                        in_=pi[half, jp][:, jj].rearrange("q m t -> q (m t)"),
                    )

        st = {}

        def u_mm(i, j):
            y = psum.tile([P, 512], F32, name="y", tag="y", bufs=2)
            ncols = slice(P * i, P * i + P)
            for g in range(2):
                nc.tensor.matmul_mx(
                    out=y[:],
                    lhsT=wq[:, g, ncols].bitcast(FP8X4),
                    lhsT_scale=wqs[:, g, ncols],
                    rhs=xq[:, j, g, :].bitcast(FP8X4),
                    rhs_scale=xqs[:, j, g, :],
                    start=(g == 0),
                    stop=(g == 1),
                )
            turns = stage.tile([P, 512], F32, name="turns", bufs=2)
            nc.scalar.activation(out=turns[:], in_=y[:], func=ACT.Identity, scale=f1[:, i : i + 1], bias=b1[:, i : i + 1])
            k = stage.tile([P, 512], I32, name="k", bufs=3)
            nc.gpsimd.tensor_scalar(k[:], turns[:], 1.0, 0.0, OP.mult, OP.add)
            st[i, j] = (y, k)

        def u_sin(i, j):
            y, k = st[i, j]
            r = stage.tile([P, 512], F32, name="r", bufs=2)
            nc.vector.scalar_tensor_tensor(r[:], y[:], f1[:, i : i + 1], k[:], OP.mult, OP.subtract)
            s = stage.tile([P, 512], F32, name="s", bufs=3)
            nc.scalar.activation(out=s[:], in_=r[:], func=ACT.Sin, scale=TWO_PI, bias=fb1[:, i : i + 1])
            st[i, j] = s

        hi = {}

        def u_turn(i, j):
            s = st[i, j]
            th = psum.tile([P, PACK, P], F32, name="th", tag="th", bufs=1)
            for t in range(PACK):
                nc.tensor.transpose(th[:, t, :], s[:, t * P : (t + 1) * P], ident_f[:])
            hi[i, j] = stage.tile([P, P, PACK], BF16, name="hi", align_bytes=64, bufs=3)
            nc.vector.tensor_tensor(
                hi[i, j][:],
                th[:].rearrange("q t n -> q n t"),
                amp_sb[:, j, :].unsqueeze(1).to_broadcast([P, P, PACK]),
                OP.mult,
            )

        def u_quant(i, j):
            ncols = slice(P * i, P * i + P)
            nc.vector.quantize_mx(
                out=hq[:, j, ncols].bitcast(FP8X4),
                scales=hqs[:, j, ncols],
                in_=hi[i, j][:].rearrange("q n t -> q (n t)"),
            )

        zs = {}

        def z_mm(i, half):
            z = psum.tile([P, 512], F32, name="z", tag="z", bufs=2)
            ncols = slice(P * i, P * i + P)
            rcols = slice(512 * half, 512 * half + 512)
            for j in range(4):
                nc.tensor.matmul_mx(
                    out=z[:],
                    lhsT=hq[:, j, ncols].bitcast(FP8X4),
                    lhsT_scale=hqs[:, j, ncols],
                    rhs=pq[:, j, rcols].bitcast(FP8X4),
                    rhs_scale=pqs[:, j, rcols],
                    start=(j == 0),
                    stop=(j == 3),
                )
            zs[i, half] = z

        def z_red(i, half):
            turns2 = stage.tile([P, 512], F32, name="turns2", bufs=2)
            nc.scalar.activation(out=turns2[:], in_=zs[i, half][:], func=ACT.Identity, scale=f2[:, i : i + 1], bias=b2[:, i : i + 1])
            k2 = stage.tile([P, 512], I32, name="k2", bufs=2)
            nc.vector.tensor_copy(out=k2[:], in_=turns2[:])
            r2 = stage.tile([P, 512], F32, name="r2", bufs=2)
            nc.vector.tensor_tensor(r2[:], turns2[:], k2[:], OP.subtract)
            zs[i, half] = r2

        def z_out(i, half):
            r2 = zs[i, half]
            ob = psum.tile([P, PACK, P], F32, name="ob", tag="tx", bufs=3)
            for q in range(4):
                nc.tensor.transpose(ob[:, q, :], r2[:, q * P : (q + 1) * P], ident_f[:])
            o = stage.tile([P, PACK, P], F32, name="o", bufs=3)
            nc.scalar.activation(out=o[:], in_=ob[:], func=ACT.Sin, scale=TWO_PI)
            nc.sync.dma_start(
                out=out[512 * half : 512 * half + 512, P * i : P * i + P].rearrange("(a q) n -> q a n", q=P),
                in_=o[:],
            )

        units = [(i, j) for j in range(4) for i in range(GROUP0)] + [(i, j) for i in range(GROUP0, 8) for j in range(4)]
        z_tasks = [(i, h) for i in range(8) for h in range(2)]
        p_tasks = [(h, jp, rr) for h in range(2) for jp in range(2) for rr in range(4)]
        at = {u: s for s, u in enumerate(units)}

        for q in range(4):
            w_prep(q)
        for t in range(4):
            x_mult(0, t)
            x_turn(0, t)
        x_quant(0, 0)
        x_quant(0, 1)

        z_next = 0
        z_log = {}
        s = 0
        while s < len(units) + 4 or z_next < len(z_tasks) or (s - 1) in z_log or (s - 2) in z_log:
            if 0 <= s - 1 < 32:
                u_sin(*units[s - 1])
            if 0 <= s - 2 < 32:
                u_turn(*units[s - 2])
            if s - 2 in z_log:
                z_out(*z_log[s - 2])
            if s < 16 and s // 4 + 1 < 4:
                x_mult(s // 4 + 1, s % 4)
                x_turn(s // 4 + 1, s % 4)
                if s % 4 == 3:
                    x_quant(s // 4 + 1, 0)
                    x_quant(s // 4 + 1, 1)
            if 2 <= s < 18:
                p_turn(*p_tasks[s - 2])
            if 0 <= s - 3 < 32:
                u_quant(*units[s - 3])
            if s - 1 in z_log:
                z_red(*z_log[s - 1])
            if s < 32:
                u_mm(*units[s])
            if z_next < 16 and s >= 18 and at[z_tasks[z_next][0], 3] + 4 <= s:
                z_log[s] = z_tasks[z_next]
                z_mm(*z_log[s])
                z_next += 1
            s += 1
